import numpy as np
import ml_dtypes


def mxq(x, axis, fmt="e4m3"):
    dtype, down = {"e4m3": (ml_dtypes.float8_e4m3fn, 7), "e5m2": (ml_dtypes.float8_e5m2, 14)}[fmt]
    v = np.moveaxis(np.asarray(x, np.float32).astype(ml_dtypes.bfloat16).astype(np.float64), axis, -1)
    blocks = v.reshape(v.shape[:-1] + (-1, 32))
    amax = np.abs(blocks).max(-1, keepdims=True)
    byte = np.maximum(np.where(amax > 0, np.frexp(amax)[1] - 1 + 127, 0) - down, 1)
    scale = np.exp2(byte - 127.0)
    codes = (blocks / scale).astype(np.float32).astype(dtype).astype(np.float64)
    return np.moveaxis((codes * scale).reshape(v.shape), -1, axis)


WIDE = False


def mx_kscale(k):
    if not WIDE:
        return np.ones(k)
    levels = np.array([10, -10, 5, -5, 0])
    if k % 512:
        return np.exp2(np.random.permutation(np.resize(levels, k // 32))).repeat(32)
    a = np.empty((k // 512, 16))
    for p in range(k // 512):
        a[p, :8] = np.random.permutation(np.resize(levels, 8))
        for g in range(8):
            far = levels[np.abs(levels - a[p, g]) >= 10]
            a[p, g + 8] = far[np.random.randint(len(far))]
    return np.exp2(a.ravel()).repeat(32)


BF16 = ml_dtypes.bfloat16


def bf(x):
    return np.asarray(x, np.float32).astype(BF16)


def f64(x):
    return np.asarray(x).astype(np.float64)


E2M1 = np.array([0.0, 0.5, 1.0, 1.5, 2.0, 3.0, 4.0, 6.0, -0.0, -0.5, -1.0, -1.5, -2.0, -3.0, -4.0, -6.0])


def pack_weight(w, fmt):
    k, n = w.shape
    w = f64(bf(w)).reshape(k // 32, 32, n)
    amax = np.abs(w).max(1)
    if fmt == "e4m3":
        byte = np.frexp(amax)[1] - 1 + 127 - 7
    else:
        mant, ex = np.frexp(amax / 6.0)
        byte = np.where(mant > 0.5, ex, ex - 1) + 127
    byte = np.clip(np.where(amax > 0, byte, 1), 1, 254)
    scaled = (w * np.exp2(127.0 - byte)[:, None, :]).reshape(k, n).astype(np.float32)
    by_word = np.ascontiguousarray(scaled.reshape(k // 512, 128, 4, n).transpose(0, 1, 3, 2))
    if fmt == "e4m3":
        words = by_word.astype(ml_dtypes.float8_e4m3fn).view(np.uint8)
    else:
        c = by_word.astype(ml_dtypes.float4_e2m1fn).view(np.uint8) & 0xF
        words = c[..., 0::2] | (c[..., 1::2] << 4)
    return np.ascontiguousarray(words), np.ascontiguousarray(byte.astype(np.uint8).reshape(k // 512, 16, n))


def unpack_weight(words, scales, fmt):
    g, p, n, _ = words.shape
    if fmt == "e4m3":
        vals = np.ascontiguousarray(words).view(ml_dtypes.float8_e4m3fn).astype(np.float64)
    else:
        nib = np.empty((g, p, n, 4), np.uint8)
        nib[..., 0::2] = words & 0xF
        nib[..., 1::2] = words >> 4
        vals = E2M1[nib]
    vals = vals * np.repeat(np.exp2(scales.astype(np.float64) - 127.0), 8, axis=1)[..., None]
    return vals.transpose(0, 1, 3, 2).reshape(g * 512, n)
def pack4(w):
    words, scales = pack_weight(w, "e2m1")
    return words.reshape(words.shape[0], 128, -1), scales


def unpack4(words, scales):
    return unpack_weight(words.reshape(words.shape[0], 128, -1, 2), scales, "e2m1")


B, I, R, C = 1024, 2048, 1024, 512


def draw0():
    s, t, u = mx_kscale(I), mx_kscale(R), mx_kscale(B)
    W = np.random.standard_normal((R, I)) / np.sqrt(R) / t[:, None]
    dec_words, dec_scales = pack4(W)
    return {
        "x": bf(np.random.standard_normal((B, I)) * s * u[:, None]),
        "enc": bf(np.random.standard_normal((I, R)) / np.sqrt(I) / s[:, None]),
        "gain": bf((1 + 0.1 * np.random.standard_normal(R)) * t),
        "dec_words": dec_words,
        "dec_scales": dec_scales,
        "diag": bf((0.5 + 0.1 * np.random.standard_normal(I)) / s),
        "mix": bf(np.random.standard_normal((C, B)) / np.sqrt(B) / u),
    }


def core(x, enc, gain, dec_words, dec_scales, diag, mix):
    x = f64(x)
    h = (mxq(x, 1, "e4m3") @ mxq(f64(enc), 0, "e4m3")) * f64(gain)
    W = unpack4(dec_words, dec_scales)
    scores = (mxq(h, 1, "e4m3") @ W) - x * f64(diag)
    profiles = mxq(f64(mix), 1, "e4m3") @ mxq(h, 0, "e4m3")
    return scores, profiles


def e4m3fn_bytes(y):
    return np.clip(np.asarray(y, np.float64), -448.0, 448.0).astype(np.float32).astype(ml_dtypes.float8_e4m3fn).view(np.uint8)


def e4m3fn_values(b):
    return np.asarray(b, np.uint8).view(ml_dtypes.float8_e4m3fn).astype(np.float64)


def setup_inputs():
    d = draw0()
    x0 = np.asarray(d['enc']).astype(np.float64)
    s = (np.max(np.abs(x0), axis=(1,), keepdims=True) / 448.0).astype(np.float32)
    out = {}
    for k, v in d.items():
        if k == 'enc':
            out['enc_bytes'] = e4m3fn_bytes(x0 / s.astype(np.float64))
            out['enc_scale'] = s
        else:
            out[k] = v
    return out


def reference(x, enc_bytes, enc_scale, gain, dec_words, dec_scales, diag, mix):
    return core(x, e4m3fn_values(enc_bytes) * enc_scale.astype(np.float64), gain, dec_words, dec_scales, diag, mix)

@@ -1,0 +1,403 @@
+from contextlib import ExitStack
+
+import concourse.mybir as mybir
+from concourse.masks import make_identity
+
+P = 128
+B, I, R, C = 1024, 2048, 1024, 512
+K_PASS = 512
+N_TILE = 512
+FLOPS = 2 * (B * I * R + B * R * I + C * B * R)
+
+F32 = mybir.dt.float32
+BF16 = mybir.dt.bfloat16
+I32 = mybir.dt.int32
+U32 = mybir.dt.uint32
+U8 = mybir.dt.uint8
+FP8 = mybir.dt.float8_e4m3fn
+FP8X4 = mybir.dt.float8_e4m3fn_x4
+FP4X4 = mybir.dt.float4_e2m1fn_x4
+MULT = mybir.AluOpType.mult
+SUB = mybir.AluOpType.subtract
+COPY = mybir.ActivationFunctionType.Copy
+
+GX = 1280
+ENC_SCALAR_PLANES = (3, 2)
+
+
+def tile_lowrank_diagonal_recommender_s8_kernel(
+    tc, x, enc_bytes, enc_scale, gain, dec_words, dec_scales, diag, mix, scores, profiles
+):
+    nc = tc.nc
+    with ExitStack() as ctx:
+        keep = ctx.enter_context(tc.tile_pool(name="keep", bufs=1))
+        wide_pool = ctx.enter_context(tc.tile_pool(name="wide_pool", bufs=3))
+        grp_pool = ctx.enter_context(tc.tile_pool(name="grp_pool", bufs=4))
+        xg_pool = ctx.enter_context(tc.tile_pool(name="xg_pool", bufs=4))
+        out_pool = ctx.enter_context(tc.tile_pool(name="out_pool", bufs=4))
+        prof_pool = ctx.enter_context(tc.tile_pool(name="prof_pool", bufs=2))
+        mm_psum = ctx.enter_context(tc.psum_pool(name="mm_psum", bufs=4))
+        tr_psum = ctx.enter_context(tc.psum_pool(name="tr_psum", bufs=4))
+
+        ident = keep.tile([P, P], F32, name="ident")
+        warm = keep.tile([P, 1], F32, name="warm")
+        es = keep.tile([P, 4, 4], F32, name="es")
+        gain_b = keep.tile([P, 2, 4], BF16, name="gain_b")
+        gain_f = keep.tile([P, 2, 4], F32, name="gain_f")
+        diag_b = keep.tile([P, I], BF16, name="diag_b")
+        encb = [keep.tile([P, 4, R], U8, name=f"encb{g}", align_bytes=64) for g in range(4)]
+        xt = [keep.tile([P, I], BF16, name=f"xt{b}", align_bytes=64) for b in range(8)]
+        mixt = keep.tile([P, 4, B], BF16, name="mixt", align_bytes=64)
+        encq = keep.tile([P, 4, R], U32, name="encq", align_bytes=64)
+        encs = keep.tile([P, 4, R], U8, name="encs", align_bytes=64)
+        xq = keep.tile([P, 4, B], U32, name="xq", align_bytes=64)
+        xs = keep.tile([P, 4, B], U8, name="xs", align_bytes=64)
+        hb = [[keep.tile([P, 4, 512], BF16, name=f"hb{c}{h}", align_bytes=64) for h in range(2)] for c in range(2)]
+        hq = keep.tile([P, 2, B], U32, name="hq", align_bytes=64)
+        hs = keep.tile([P, 2, B], U8, name="hs", align_bytes=64)
+        pq = keep.tile([P, 2, R], U32, name="pq", align_bytes=64)
+        ps = keep.tile([P, 2, R], U8, name="ps", align_bytes=64)
+        mq = keep.tile([P, 2, C], U32, name="mq", align_bytes=64)
+        ms = keep.tile([P, 2, C], U8, name="ms", align_bytes=64)
+        ww = keep.tile([P, 2, 2 * I], U8, name="ww", align_bytes=64)
+        ws = keep.tile([P, 2, I], U8, name="ws", align_bytes=64)
+
+        nc.scalar.dma_start(out=es[:], in_=enc_scale.rearrange("(g p t) o -> p g (t o)", p=P, t=4))
+        nc.scalar.dma_start(out=gain_b[:], in_=gain.rearrange("(h p t) -> p h t", p=P, t=4))
+        enc_v = enc_bytes.rearrange("(g p t) n -> g p t n", p=P, t=4)
+
+        def load_enc(g):
+            nc.sync.dma_start(out=encb[g][:], in_=enc_v[g])
+
+        def load_x(b):
+            nc.sync.dma_start(out=xt[b][:], in_=x[b * P : (b + 1) * P, :])
+
+        load_enc(0)
+        load_x(0)
+        load_x(1)
+        load_enc(1)
+        load_x(2)
+        load_x(3)
+        load_enc(2)
+        load_enc(3)
+        for b in range(4, 8):
+            load_x(b)
+        nc.sync.dma_start(out=ww[:], in_=dec_words.rearrange("g p n -> p g n"))
+        nc.gpsimd.memset(ws[:].rearrange("p g n -> p (g n)").bitcast(I32), 0)
+        make_identity(nc, ident[:])
+        ws_words = ws[:].rearrange("p g n -> p (g n)").bitcast(I32)
+        for r in range(4):
+            nc.sync.dma_start(
+                out=ws_words[r:P:32, :].rearrange("q (g n) -> q g n", g=2),
+                in_=dec_scales.rearrange("g (q r) n -> r q g n", r=4)[r].bitcast(I32),
+            )
+        nc.sync.dma_start(out=diag_b[:], in_=diag.partition_broadcast(P))
+        nc.sync.dma_start(out=mixt[:], in_=mix.rearrange("(c p) b -> p c b", p=P))
+
+        nc.vector.memset(warm[:], 0.0)
+        nc.scalar.activation(out=warm[:], in_=warm[:], func=COPY, scale=1.0)
+        nc.vector.tensor_copy(out=gain_f[:], in_=gain_b[:])
+
+        wide = {}
+        grouped = {}
+
+        def widen_plane(h, g, j, engine_is_scalar):
+            src = encb[g][:, j, h * 512 : (h + 1) * 512].bitcast(FP8)
+            dst = wide[h, g][:, j, :]
+            if engine_is_scalar:
+                nc.scalar.activation(out=dst, in_=src, func=COPY, scale=es[:, g, j : j + 1])
+            else:
+                nc.vector.tensor_scalar(out=dst, in0=src, scalar1=es[:, g, j : j + 1], scalar2=None, op0=MULT)
+
+        def widen(h, g):
+            wide[h, g] = wide_pool.tile([P, 4, 512], BF16, name="wide", align_bytes=64)
+            for j in range(4):
+                widen_plane(h, g, j, j < ENC_SCALAR_PLANES[h])
+
+        def interleave_enc(h, g):
+            grouped["e", h, g] = grp_pool.tile([P, 512, 4], BF16, name="grp", align_bytes=64)
+            nc.vector.tensor_copy(
+                out=grouped["e", h, g][:].rearrange("p (t m) j -> p m j t", t=4),
+                in_=wide[h, g][:].rearrange("p j (m t) -> p m j t", t=4),
+            )
+
+        def quant_enc(h, g):
+            nc.vector.quantize_mx(
+                out=encq[:, g, h * 512 : (h + 1) * 512].bitcast(FP8X4),
+                scales=encs[:, g, h * 512 : (h + 1) * 512],
+                in_=grouped["e", h, g][:].rearrange("p n j -> p (n j)"),
+            )
+
+        banks = {}
+        xg = {}
+
+        def tx(q, g):
+            banks["x", q, g] = tr_psum.tile([P, 2, 2, P], F32, name="tr")
+            for k in range(2):
+                words = xt[2 * q + k][:].bitcast(F32)
+                for u in range(2):
+                    nc.tensor.transpose(
+                        banks["x", q, g][:, k, u, :], words[:, 256 * g + u : 256 * (g + 1) : 2], ident[:]
+                    )
+
+        def evac_x(q, g):
+            xg[q, g] = xg_pool.tile([P, 256, 4], BF16, name="xg", align_bytes=64)
+            nc.scalar.copy(
+                out=xg[q, g][:].rearrange("p (k r) t -> p k (r t)", k=2).bitcast(F32).rearrange("p k (r u) -> p k r u", u=2),
+                in_=banks["x", q, g][:].rearrange("p k u r -> p k r u"),
+            )
+
+        def quant_x(q, g):
+            nc.vector.quantize_mx(
+                out=xq[:, g, q * 256 : (q + 1) * 256].bitcast(FP8X4),
+                scales=xs[:, g, q * 256 : (q + 1) * 256],
+                in_=xg[q, g][:].rearrange("p n j -> p (n j)"),
+            )
+
+        h_ps = {}
+
+        def h_pass(c, h, t, g):
+            if g == 0:
+                h_ps[c, h, t] = mm_psum.tile([P, N_TILE], F32, name="mm")
+            lo = h * 512 + t * P
+            nc.tensor.matmul_mx(
+                out=h_ps[c, h, t][:],
+                lhsT=encq[:, g, lo : lo + P].bitcast(FP8X4),
+                lhsT_scale=encs[:, g, lo : lo + P],
+                rhs=xq[:, g, c * 512 : (c + 1) * 512].bitcast(FP8X4),
+                rhs_scale=xs[:, g, c * 512 : (c + 1) * 512],
+                start=(g == 0),
+                stop=(g == 3),
+            )
+
+        def evac_h(c, h, t):
+            nc.scalar.activation(
+                out=hb[c][h][:, t, :], in_=h_ps[c, h, t][:], func=COPY, scale=gain_f[:, h, t : t + 1]
+            )
+
+        def interleave_h(c, h):
+            grouped["h", c, h] = grp_pool.tile([P, 512, 4], BF16, name="grp", align_bytes=64)
+            nc.vector.tensor_copy(
+                out=grouped["h", c, h][:].rearrange("p (k i) t -> p k t i", i=4),
+                in_=hb[c][h][:].rearrange("p t (k i) -> p k t i", i=4),
+            )
+
+        def quant_h(c, h):
+            nc.vector.quantize_mx(
+                out=hq[:, h, c * 512 : (c + 1) * 512].bitcast(FP8X4),
+                scales=hs[:, h, c * 512 : (c + 1) * 512],
+                in_=grouped["h", c, h][:].rearrange("p n j -> p (n j)"),
+            )
+
+        def tp(c, h, k):
+            banks["p", c, h, k] = tr_psum.tile([P, 2, 2, P], F32, name="tr")
+            for i in range(2):
+                words = hb[c][h][:, 2 * k + i, :].bitcast(F32)
+                for u in range(2):
+                    nc.tensor.transpose(banks["p", c, h, k][:, i, u, :], words[:, u:256:2], ident[:])
+
+        def evac_p(c, h, k):
+            if k == 0:
+                grouped["p", c, h] = grp_pool.tile([P, 512, 4], BF16, name="grp", align_bytes=64)
+            half = grouped["p", c, h][:, k * 256 : (k + 1) * 256, :]
+            nc.scalar.copy(
+                out=half.rearrange("p n t -> p (n t)").bitcast(F32).rearrange("p (i r u) -> p i r u", i=2, u=2),
+                in_=banks["p", c, h, k][:].rearrange("p i u r -> p i r u"),
+            )
+
+        def quant_p(c, h):
+            nc.vector.quantize_mx(
+                out=pq[:, c, h * 512 : (h + 1) * 512].bitcast(FP8X4),
+                scales=ps[:, c, h * 512 : (h + 1) * 512],
+                in_=grouped["p", c, h][:].rearrange("p n j -> p (n j)"),
+            )
+
+        def tm(c, k):
+            banks["m", c, k] = tr_psum.tile([P, 2, 2, P], F32, name="tr")
+            for i in range(2):
+                words = mixt[:, 2 * k + i, :].bitcast(F32)
+                for u in range(2):
+                    nc.tensor.transpose(
+                        banks["m", c, k][:, i, u, :], words[:, 256 * c + u : 256 * (c + 1) : 2], ident[:]
+                    )
+
+        def evac_m(c, k):
+            if k == 0:
+                grouped["m", c] = grp_pool.tile([P, 512, 4], BF16, name="grp", align_bytes=64)
+            half = grouped["m", c][:, k * 256 : (k + 1) * 256, :]
+            nc.scalar.copy(
+                out=half.rearrange("p n t -> p (n t)").bitcast(F32).rearrange("p (i r u) -> p i r u", i=2, u=2),
+                in_=banks["m", c, k][:].rearrange("p i u r -> p i r u"),
+            )
+
+        def quant_m(c):
+            nc.vector.quantize_mx(
+                out=mq[:, c, :].bitcast(FP8X4),
+                scales=ms[:, c, :],
+                in_=grouped["m", c][:].rearrange("p n j -> p (n j)"),
+            )
+
+        ot = {}
+
+        def diag_term(b):
+            ot[b] = out_pool.tile([P, I], F32, name="ot", align_bytes=64)
+            nc.gpsimd.tensor_tensor(out=ot[b][:, :GX], in0=xt[b][:, :GX], in1=diag_b[:, :GX], op=MULT)
+            nc.vector.tensor_tensor(out=ot[b][:, GX:], in0=xt[b][:, GX:], in1=diag_b[:, GX:], op=MULT)
+
+        s_ps = {}
+
+        def score_mm(b, n):
+            s_ps[b, n] = mm_psum.tile([P, N_TILE], F32, name="mm")
+            cols = slice(n * N_TILE, (n + 1) * N_TILE)
+            for h in range(2):
+                nc.tensor.matmul_mx(
+                    out=s_ps[b, n][:],
+                    lhsT=hq[:, h, b * P : (b + 1) * P].bitcast(FP8X4),
+                    lhsT_scale=hs[:, h, b * P : (b + 1) * P],
+                    rhs=ww[:, h, n * 2 * N_TILE : (n + 1) * 2 * N_TILE].bitcast(FP4X4),
+                    rhs_scale=ws[:, h, cols],
+                    start=(h == 0),
+                    stop=(h == 1),
+                )
+
+        def score_out(b, n):
+            cols = slice(n * N_TILE, (n + 1) * N_TILE)
+            nc.vector.tensor_tensor(out=ot[b][:, cols], in0=s_ps[b, n][:], in1=ot[b][:, cols], op=SUB)
+
+        def score_store(b, lo, hi):
+            nc.sync.dma_start(out=scores[b * P : (b + 1) * P, lo:hi], in_=ot[b][:, lo:hi])
+
+        p_ps = {}
+        pt = {}
+
+        def profile_mm(m, h):
+            p_ps[m, h] = mm_psum.tile([P, N_TILE], F32, name="mm")
+            for c in range(2):
+                nc.tensor.matmul_mx(
+                    out=p_ps[m, h][:],
+                    lhsT=mq[:, c, m * P : (m + 1) * P].bitcast(FP8X4),
+                    lhsT_scale=ms[:, c, m * P : (m + 1) * P],
+                    rhs=pq[:, c, h * 512 : (h + 1) * 512].bitcast(FP8X4),
+                    rhs_scale=ps[:, c, h * 512 : (h + 1) * 512],
+                    start=(c == 0),
+                    stop=(c == 1),
+                )
+
+        def profile_out(m, h):
+            if h == 0:
+                pt[m] = prof_pool.tile([P, R], F32, name="pt", align_bytes=64)
+            nc.scalar.copy(
+                out=pt[m][:, h * 512 : (h + 1) * 512].rearrange("p (r t) -> p r t", t=4),
+                in_=p_ps[m, h][:].rearrange("p (t r) -> p r t", t=4),
+            )
+            if h == 1:
+                nc.sync.dma_start(out=profiles[m * P : (m + 1) * P, :], in_=pt[m][:])
+
+        widen(0, 0)
+        for g in range(4):
+            tx(0, g)
+            evac_x(0, g)
+        interleave_enc(0, 0)
+        quant_x(0, 0)
+        quant_enc(0, 0)
+        widen(0, 1)
+        quant_x(0, 1)
+        quant_x(0, 2)
+        interleave_enc(0, 1)
+        quant_x(0, 3)
+        quant_enc(0, 1)
+        widen(0, 2)
+        for g in range(4):
+            tx(1, g)
+            evac_x(1, g)
+        quant_x(1, 0)
+        interleave_enc(0, 2)
+        quant_x(1, 1)
+        quant_enc(0, 2)
+        widen(0, 3)
+        quant_x(1, 2)
+        interleave_enc(0, 3)
+        quant_x(1, 3)
+        quant_enc(0, 3)
+        for g in range(4):
+            for t in range(4):
+                h_pass(0, 0, t, g)
+            if g == 2:
+                for k in range(4):
+                    tx(2, k)
+                    evac_x(2, k)
+
+        for t in range(4):
+            evac_h(0, 0, t)
+        widen(1, 0)
+        for k in range(4):
+            tx(3, k)
+            evac_x(3, k)
+        for g in range(4):
+            quant_x(2, g)
+        interleave_h(0, 0)
+        interleave_enc(1, 0)
+        quant_h(0, 0)
+        quant_enc(1, 0)
+        widen(1, 1)
+        for g in range(4):
+            quant_x(3, g)
+        for t in range(4):
+            for g in range(4):
+                h_pass(1, 0, t, g)
+            evac_h(1, 0, t)
+        interleave_enc(1, 1)
+        widen(1, 2)
+        quant_enc(1, 1)
+        interleave_enc(1, 2)
+        interleave_h(1, 0)
+        quant_enc(1, 2)
+        widen(1, 3)
+        quant_h(1, 0)
+        interleave_enc(1, 3)
+        diag_term(0)
+        quant_enc(1, 3)
+        for g in range(4):
+            for t in range(4):
+                h_pass(0, 1, t, g)
+        for t in range(4):
+            evac_h(0, 1, t)
+        diag_term(1)
+        for t in range(4):
+            for g in range(4):
+                h_pass(1, 1, t, g)
+            evac_h(1, 1, t)
+        interleave_h(0, 1)
+        diag_term(2)
+        quant_h(0, 1)
+
+        extra = {
+            0: [(tp, evac_p, (0, 0)), (tp, evac_p, (1, 0))],
+            1: [(tp, evac_p, (0, 1)), (tp, evac_p, (1, 1))],
+            2: [(tm, evac_m, (0,)), (tm, evac_m, (1,))],
+        }
+        late_quant = {0: [(quant_p, (0, 0)), (quant_p, (1, 0))], 1: [(quant_p, (0, 1)), (quant_p, (1, 1))], 2: [(quant_m, (0,)), (quant_m, (1,))]}
+        for b in range(8):
+            for n in range(4):
+                score_mm(b, n)
+                score_out(b, n)
+                if b == 0 and n == 1:
+                    interleave_h(1, 1)
+                if b == 0 and n == 3:
+                    quant_h(1, 1)
+                if b == 7:
+                    score_store(b, n * 512, (n + 1) * 512)
+                elif n % 2 == 1:
+                    score_store(b, (n - 1) * 512, (n + 1) * 512)
+            for transpose, evac, args in extra.get(b, []):
+                for k in range(2):
+                    transpose(*args, k)
+                    evac(*args, k)
+            if b + 3 < 8:
+                diag_term(b + 3)
+            for quant, args in late_quant.get(b, []):
+                quant(*args)
+            if 3 <= b < 7:
+                for h in range(2):
+                    profile_mm(b - 3, h)
+                    profile_out(b - 3, h)

@@ -21,7 +21,6 @@ MULT = mybir.AluOpType.mult
 SUB = mybir.AluOpType.subtract
 COPY = mybir.ActivationFunctionType.Copy
 
-GX = 1280
 ENC_SCALAR_PLANES = (3, 2)
 
 
@@ -31,13 +30,14 @@ def tile_lowrank_diagonal_recommender_s8_kernel(
     nc = tc.nc
     with ExitStack() as ctx:
         keep = ctx.enter_context(tc.tile_pool(name="keep", bufs=1))
-        wide_pool = ctx.enter_context(tc.tile_pool(name="wide_pool", bufs=3))
+        wide_pool = ctx.enter_context(tc.tile_pool(name="wide_pool", bufs=4))
         grp_pool = ctx.enter_context(tc.tile_pool(name="grp_pool", bufs=4))
         xg_pool = ctx.enter_context(tc.tile_pool(name="xg_pool", bufs=4))
         out_pool = ctx.enter_context(tc.tile_pool(name="out_pool", bufs=4))
-        prof_pool = ctx.enter_context(tc.tile_pool(name="prof_pool", bufs=2))
-        mm_psum = ctx.enter_context(tc.psum_pool(name="mm_psum", bufs=4))
-        tr_psum = ctx.enter_context(tc.psum_pool(name="tr_psum", bufs=4))
+        prof_pool = ctx.enter_context(tc.tile_pool(name="prof_pool", bufs=4))
+        mm_psum = ctx.enter_context(tc.psum_pool(name="mm_psum", bufs=5))
+        tr_psum = ctx.enter_context(tc.psum_pool(name="tr_psum", bufs=3))
+        ctx.enter_context(tc.manual_schedule())
 
         ident = keep.tile([P, P], F32, name="ident")
         warm = keep.tile([P, 1], F32, name="warm")
@@ -102,6 +102,8 @@ def tile_lowrank_diagonal_recommender_s8_kernel(
         grouped = {}
 
         def widen_plane(h, g, j, engine_is_scalar):
+            if (h, g) not in wide:
+                wide[h, g] = wide_pool.tile([P, 4, 512], BF16, name="wide", align_bytes=64)
             src = encb[g][:, j, h * 512 : (h + 1) * 512].bitcast(FP8)
             dst = wide[h, g][:, j, :]
             if engine_is_scalar:
@@ -110,13 +112,12 @@ def tile_lowrank_diagonal_recommender_s8_kernel(
                 nc.vector.tensor_scalar(out=dst, in0=src, scalar1=es[:, g, j : j + 1], scalar2=None, op0=MULT)
 
         def widen(h, g):
-            wide[h, g] = wide_pool.tile([P, 4, 512], BF16, name="wide", align_bytes=64)
             for j in range(4):
                 widen_plane(h, g, j, j < ENC_SCALAR_PLANES[h])
 
-        def interleave_enc(h, g):
+        def interleave_enc(h, g, copy):
             grouped["e", h, g] = grp_pool.tile([P, 512, 4], BF16, name="grp", align_bytes=64)
-            nc.vector.tensor_copy(
+            copy(
                 out=grouped["e", h, g][:].rearrange("p (t m) j -> p m j t", t=4),
                 in_=wide[h, g][:].rearrange("p j (m t) -> p m j t", t=4),
             )
@@ -140,9 +141,9 @@ def tile_lowrank_diagonal_recommender_s8_kernel(
                         banks["x", q, g][:, k, u, :], words[:, 256 * g + u : 256 * (g + 1) : 2], ident[:]
                     )
 
-        def evac_x(q, g):
+        def evac_x(q, g, copy):
             xg[q, g] = xg_pool.tile([P, 256, 4], BF16, name="xg", align_bytes=64)
-            nc.scalar.copy(
+            copy(
                 out=xg[q, g][:].rearrange("p (k r) t -> p k (r t)", k=2).bitcast(F32).rearrange("p k (r u) -> p k r u", u=2),
                 in_=banks["x", q, g][:].rearrange("p k u r -> p k r u"),
             )
@@ -170,14 +171,19 @@ def tile_lowrank_diagonal_recommender_s8_kernel(
                 stop=(g == 3),
             )
 
-        def evac_h(c, h, t):
-            nc.scalar.activation(
-                out=hb[c][h][:, t, :], in_=h_ps[c, h, t][:], func=COPY, scale=gain_f[:, h, t : t + 1]
-            )
+        def evac_h(c, h, t, engine_is_scalar):
+            if engine_is_scalar:
+                nc.scalar.activation(
+                    out=hb[c][h][:, t, :], in_=h_ps[c, h, t][:], func=COPY, scale=gain_f[:, h, t : t + 1]
+                )
+            else:
+                nc.vector.tensor_scalar(
+                    out=hb[c][h][:, t, :], in0=h_ps[c, h, t][:], scalar1=gain_f[:, h, t : t + 1], scalar2=None, op0=MULT
+                )
 
-        def interleave_h(c, h):
+        def interleave_h(c, h, copy):
             grouped["h", c, h] = grp_pool.tile([P, 512, 4], BF16, name="grp", align_bytes=64)
-            nc.vector.tensor_copy(
+            copy(
                 out=grouped["h", c, h][:].rearrange("p (k i) t -> p k t i", i=4),
                 in_=hb[c][h][:].rearrange("p t (k i) -> p k t i", i=4),
             )
@@ -197,7 +203,7 @@ def tile_lowrank_diagonal_recommender_s8_kernel(
                     nc.tensor.transpose(banks["p", c, h, k][:, i, u, :], words[:, u:256:2], ident[:])
 
         def evac_p(c, h, k):
-            if k == 0:
+            if ("p", c, h) not in grouped:
                 grouped["p", c, h] = grp_pool.tile([P, 512, 4], BF16, name="grp", align_bytes=64)
             half = grouped["p", c, h][:, k * 256 : (k + 1) * 256, :]
             nc.scalar.copy(
@@ -222,7 +228,7 @@ def tile_lowrank_diagonal_recommender_s8_kernel(
                     )
 
         def evac_m(c, k):
-            if k == 0:
+            if ("m", c) not in grouped:
                 grouped["m", c] = grp_pool.tile([P, 512, 4], BF16, name="grp", align_bytes=64)
             half = grouped["m", c][:, k * 256 : (k + 1) * 256, :]
             nc.scalar.copy(
@@ -239,10 +245,11 @@ def tile_lowrank_diagonal_recommender_s8_kernel(
 
         ot = {}
 
-        def diag_term(b):
-            ot[b] = out_pool.tile([P, I], F32, name="ot", align_bytes=64)
-            nc.gpsimd.tensor_tensor(out=ot[b][:, :GX], in0=xt[b][:, :GX], in1=diag_b[:, :GX], op=MULT)
-            nc.vector.tensor_tensor(out=ot[b][:, GX:], in0=xt[b][:, GX:], in1=diag_b[:, GX:], op=MULT)
+        def diag_term(b, n, engine):
+            if b not in ot:
+                ot[b] = out_pool.tile([P, I], F32, name="ot", align_bytes=64)
+            cols = slice(n * N_TILE, (n + 1) * N_TILE)
+            engine.tensor_tensor(out=ot[b][:, cols], in0=xt[b][:, cols], in1=diag_b[:, cols], op=MULT)
 
         s_ps = {}
 
@@ -284,120 +291,367 @@ def tile_lowrank_diagonal_recommender_s8_kernel(
                 )
 
         def profile_out(m, h):
-            if h == 0:
-                pt[m] = prof_pool.tile([P, R], F32, name="pt", align_bytes=64)
+            piece = prof_pool.tile([P, N_TILE], F32, name="piece", align_bytes=64)
             nc.scalar.copy(
-                out=pt[m][:, h * 512 : (h + 1) * 512].rearrange("p (r t) -> p r t", t=4),
-                in_=p_ps[m, h][:].rearrange("p (t r) -> p r t", t=4),
+                out=piece[:].rearrange("p (r t) -> p r t", t=4), in_=p_ps[m, h][:].rearrange("p (t r) -> p r t", t=4)
             )
-            if h == 1:
-                nc.sync.dma_start(out=profiles[m * P : (m + 1) * P, :], in_=pt[m][:])
+            nc.sync.dma_start(out=profiles[m * P : (m + 1) * P, h * 512 : (h + 1) * 512], in_=piece[:])
 
-        widen(0, 0)
-        for g in range(4):
-            tx(0, g)
-            evac_x(0, g)
-        interleave_enc(0, 0)
-        quant_x(0, 0)
-        quant_enc(0, 0)
-        widen(0, 1)
-        quant_x(0, 1)
-        quant_x(0, 2)
-        interleave_enc(0, 1)
+        widen_plane(0, 0, 0, False)
+        widen_plane(1, 0, 2, False)
+        widen_plane(1, 0, 1, True)
+        widen_plane(0, 0, 2, True)
+        tx(0, 3)
+        tx(0, 2)
+        widen_plane(0, 0, 3, False)
+        widen_plane(0, 0, 1, False)
+        tx(0, 0)
+        widen_plane(1, 0, 3, True)
+        widen_plane(1, 0, 0, False)
+        interleave_enc(0, 0, nc.vector.tensor_copy)
+        evac_x(0, 3, nc.vector.tensor_copy)
+        widen_plane(0, 1, 1, False)
+        widen_plane(0, 1, 2, False)
+        widen_plane(0, 1, 0, False)
         quant_x(0, 3)
-        quant_enc(0, 1)
-        widen(0, 2)
-        for g in range(4):
-            tx(1, g)
-            evac_x(1, g)
-        quant_x(1, 0)
-        interleave_enc(0, 2)
-        quant_x(1, 1)
-        quant_enc(0, 2)
-        widen(0, 3)
-        quant_x(1, 2)
-        interleave_enc(0, 3)
-        quant_x(1, 3)
-        quant_enc(0, 3)
-        for g in range(4):
-            for t in range(4):
-                h_pass(0, 0, t, g)
-            if g == 2:
-                for k in range(4):
-                    tx(2, k)
-                    evac_x(2, k)
-
-        for t in range(4):
-            evac_h(0, 0, t)
-        widen(1, 0)
-        for k in range(4):
-            tx(3, k)
-            evac_x(3, k)
-        for g in range(4):
-            quant_x(2, g)
-        interleave_h(0, 0)
-        interleave_enc(1, 0)
-        quant_h(0, 0)
+        interleave_enc(1, 0, nc.scalar.copy)
+        evac_x(0, 2, nc.scalar.copy)
         quant_enc(1, 0)
-        widen(1, 1)
-        for g in range(4):
-            quant_x(3, g)
-        for t in range(4):
-            for g in range(4):
-                h_pass(1, 0, t, g)
-            evac_h(1, 0, t)
-        interleave_enc(1, 1)
-        widen(1, 2)
+        quant_x(0, 2)
+        tx(0, 1)
+        tx(1, 3)
+        evac_x(0, 1, nc.scalar.copy)
+        evac_x(0, 0, nc.scalar.copy)
+        quant_enc(0, 0)
+        tx(1, 0)
+        evac_x(1, 3, nc.scalar.copy)
+        widen_plane(0, 2, 2, False)
+        widen_plane(1, 2, 2, False)
+        widen_plane(0, 1, 3, True)
+        quant_x(0, 1)
+        interleave_enc(0, 1, nc.vector.tensor_copy)
+        widen_plane(1, 1, 1, False)
+        widen_plane(0, 2, 0, False)
+        quant_x(0, 0)
+        widen_plane(0, 3, 0, False)
+        widen_plane(1, 1, 0, True)
+        evac_x(1, 0, nc.scalar.copy)
+        tx(1, 1)
+        evac_x(1, 1, nc.scalar.copy)
+        quant_x(1, 1)
+        quant_x(1, 3)
+        quant_x(1, 0)
+        widen_plane(0, 2, 3, False)
+        quant_enc(0, 1)
+        widen_plane(0, 3, 2, False)
+        widen_plane(0, 3, 3, True)
+        tx(2, 0)
+        widen_plane(1, 2, 0, True)
+        tx(2, 3)
+        tx(1, 2)
+        evac_x(2, 0, nc.scalar.copy)
+        widen_plane(0, 2, 1, True)
+        evac_x(2, 3, nc.scalar.copy)
+        tx(3, 0)
+        evac_x(1, 2, nc.scalar.copy)
+        tx(3, 1)
+        widen_plane(0, 3, 1, False)
+        evac_x(3, 0, nc.scalar.copy)
+        quant_x(2, 0)
+        quant_x(2, 3)
+        widen_plane(1, 1, 3, False)
+        interleave_enc(0, 2, nc.vector.tensor_copy)
+        tx(2, 2)
+        evac_x(3, 1, nc.scalar.copy)
+        quant_x(3, 0)
+        tx(3, 2)
+        tx(2, 1)
+        quant_x(1, 2)
+        interleave_enc(0, 3, nc.scalar.copy)
+        evac_x(3, 2, nc.scalar.copy)
+        widen_plane(1, 3, 0, True)
+        quant_enc(0, 2)
+        evac_x(2, 1, nc.scalar.copy)
+        quant_enc(0, 3)
+        h_pass(0, 0, 3, 0)
+        h_pass(0, 0, 0, 0)
+        h_pass(0, 0, 1, 0)
+        widen_plane(1, 2, 1, False)
+        h_pass(0, 0, 1, 1)
+        h_pass(0, 0, 2, 0)
+        widen_plane(1, 1, 2, False)
+        h_pass(0, 0, 2, 1)
+        h_pass(0, 0, 3, 1)
+        h_pass(0, 0, 0, 1)
+        h_pass(0, 0, 1, 2)
+        h_pass(0, 0, 0, 2)
+        h_pass(0, 0, 3, 2)
+        h_pass(0, 0, 1, 3)
+        diag_term(0, 0, nc.vector)
+        h_pass(0, 0, 0, 3)
+        h_pass(0, 0, 2, 2)
+        h_pass(0, 0, 3, 3)
+        quant_x(2, 1)
+        interleave_enc(1, 1, nc.vector.tensor_copy)
+        evac_x(2, 2, nc.scalar.copy)
+        h_pass(1, 0, 0, 0)
+        quant_x(3, 1)
+        evac_h(0, 0, 0, True)
+        tx(3, 3)
+        tm(1, 1)
+        evac_h(0, 0, 3, True)
+        evac_h(0, 0, 1, True)
+        evac_x(3, 3, nc.scalar.copy)
+        tm(1, 0)
+        h_pass(0, 0, 2, 3)
+        widen_plane(1, 2, 3, False)
+        widen_plane(1, 3, 1, True)
+        widen_plane(1, 3, 2, True)
+        quant_x(2, 2)
+        widen_plane(1, 3, 3, False)
+        quant_x(3, 2)
+        evac_m(1, 1)
+        evac_h(0, 0, 2, True)
+        diag_term(3, 0, nc.vector)
+        quant_x(3, 3)
+        diag_term(1, 0, nc.vector)
         quant_enc(1, 1)
-        interleave_enc(1, 2)
-        interleave_h(1, 0)
+        diag_term(1, 1, nc.vector)
+        evac_m(1, 0)
+        h_pass(1, 0, 3, 0)
+        h_pass(1, 0, 0, 1)
+        h_pass(1, 0, 2, 0)
+        h_pass(0, 1, 3, 0)
+        h_pass(1, 0, 2, 1)
+        h_pass(1, 0, 2, 2)
+        h_pass(1, 0, 0, 2)
+        h_pass(1, 0, 3, 1)
+        h_pass(1, 0, 3, 2)
+        h_pass(1, 0, 2, 3)
+        h_pass(1, 0, 1, 0)
+        h_pass(1, 0, 0, 3)
+        interleave_enc(1, 2, nc.vector.tensor_copy)
+        evac_h(1, 0, 0, False)
+        h_pass(1, 0, 3, 3)
+        evac_h(1, 0, 2, True)
+        tp(0, 0, 1)
+        tp(0, 0, 0)
+        h_pass(1, 0, 1, 1)
+        evac_h(1, 0, 3, False)
+        diag_term(0, 2, nc.gpsimd)
         quant_enc(1, 2)
-        widen(1, 3)
-        quant_h(1, 0)
-        interleave_enc(1, 3)
-        diag_term(0)
+        h_pass(1, 0, 1, 2)
+        h_pass(1, 0, 1, 3)
+        h_pass(0, 1, 3, 1)
+        h_pass(0, 1, 0, 0)
+        h_pass(0, 1, 0, 1)
+        h_pass(0, 1, 2, 0)
+        h_pass(0, 1, 3, 2)
+        h_pass(0, 1, 2, 1)
+        interleave_enc(1, 3, nc.scalar.copy)
+        interleave_h(0, 0, nc.scalar.copy)
         quant_enc(1, 3)
-        for g in range(4):
-            for t in range(4):
-                h_pass(0, 1, t, g)
-        for t in range(4):
-            evac_h(0, 1, t)
-        diag_term(1)
-        for t in range(4):
-            for g in range(4):
-                h_pass(1, 1, t, g)
-            evac_h(1, 1, t)
-        interleave_h(0, 1)
-        diag_term(2)
+        diag_term(2, 3, nc.vector)
+        quant_m(1)
+        h_pass(0, 1, 0, 2)
+        h_pass(0, 1, 3, 3)
+        h_pass(0, 1, 0, 3)
+        h_pass(0, 1, 1, 0)
+        h_pass(0, 1, 2, 2)
+        h_pass(0, 1, 1, 1)
+        h_pass(0, 1, 1, 2)
+        h_pass(0, 1, 2, 3)
+        diag_term(3, 2, nc.vector)
+        evac_h(1, 0, 1, False)
+        evac_h(0, 1, 3, True)
+        diag_term(3, 1, nc.gpsimd)
+        h_pass(1, 1, 1, 0)
+        h_pass(0, 1, 1, 3)
+        h_pass(1, 1, 0, 0)
+        h_pass(1, 1, 1, 1)
+        evac_h(0, 1, 2, False)
+        evac_h(0, 1, 0, True)
+        h_pass(1, 1, 0, 1)
+        diag_term(0, 3, nc.vector)
+        h_pass(1, 1, 3, 0)
+        h_pass(1, 1, 2, 0)
+        h_pass(1, 1, 2, 1)
+        h_pass(1, 1, 2, 2)
+        h_pass(1, 1, 2, 3)
+        h_pass(1, 1, 0, 2)
+        h_pass(1, 1, 1, 2)
+        h_pass(1, 1, 1, 3)
+        h_pass(1, 1, 3, 1)
+        h_pass(1, 1, 3, 2)
+        h_pass(1, 1, 3, 3)
+        evac_p(0, 0, 1)
+        evac_h(0, 1, 1, True)
+        quant_h(0, 0)
+        evac_p(0, 0, 0)
+        interleave_h(1, 0, nc.scalar.copy)
+        h_pass(1, 1, 0, 3)
+        interleave_h(0, 1, nc.vector.tensor_copy)
+        evac_h(1, 1, 1, True)
+        diag_term(3, 3, nc.vector)
         quant_h(0, 1)
-
-        extra = {
-            0: [(tp, evac_p, (0, 0)), (tp, evac_p, (1, 0))],
-            1: [(tp, evac_p, (0, 1)), (tp, evac_p, (1, 1))],
-            2: [(tm, evac_m, (0,)), (tm, evac_m, (1,))],
-        }
-        late_quant = {0: [(quant_p, (0, 0)), (quant_p, (1, 0))], 1: [(quant_p, (0, 1)), (quant_p, (1, 1))], 2: [(quant_m, (0,)), (quant_m, (1,))]}
-        for b in range(8):
-            for n in range(4):
-                score_mm(b, n)
-                score_out(b, n)
-                if b == 0 and n == 1:
-                    interleave_h(1, 1)
-                if b == 0 and n == 3:
-                    quant_h(1, 1)
-                if b == 7:
-                    score_store(b, n * 512, (n + 1) * 512)
-                elif n % 2 == 1:
-                    score_store(b, (n - 1) * 512, (n + 1) * 512)
-            for transpose, evac, args in extra.get(b, []):
-                for k in range(2):
-                    transpose(*args, k)
-                    evac(*args, k)
-            if b + 3 < 8:
-                diag_term(b + 3)
-            for quant, args in late_quant.get(b, []):
-                quant(*args)
-            if 3 <= b < 7:
-                for h in range(2):
-                    profile_mm(b - 3, h)
-                    profile_out(b - 3, h)
+        evac_h(1, 1, 0, True)
+        score_mm(0, 3)
+        score_mm(0, 0)
+        evac_h(1, 1, 3, True)
+        evac_h(1, 1, 2, True)
+        quant_p(0, 0)
+        quant_h(1, 0)
+        score_out(0, 3)
+        score_store(0, 1536, 2048)
+        score_out(0, 0)
+        score_store(0, 0, 512)
+        diag_term(0, 1, nc.gpsimd)
+        diag_term(2, 1, nc.gpsimd)
+        score_mm(3, 1)
+        score_mm(0, 1)
+        score_mm(0, 2)
+        score_mm(3, 3)
+        diag_term(1, 3, nc.gpsimd)
+        score_out(3, 1)
+        score_store(3, 512, 1024)
+        score_out(0, 1)
+        score_store(0, 512, 1024)
+        diag_term(1, 2, nc.gpsimd)
+        score_out(0, 2)
+        score_store(0, 1024, 1536)
+        score_out(3, 3)
+        score_store(3, 1536, 2048)
+        score_mm(1, 0)
+        score_out(1, 0)
+        score_store(1, 0, 512)
+        diag_term(2, 2, nc.gpsimd)
+        score_mm(3, 0)
+        score_mm(2, 3)
+        score_mm(3, 2)
+        score_out(2, 3)
+        score_store(2, 1536, 2048)
+        score_out(3, 0)
+        score_store(3, 0, 512)
+        diag_term(2, 0, nc.gpsimd)
+        score_mm(2, 0)
+        score_mm(2, 2)
+        score_mm(1, 2)
+        score_out(3, 2)
+        score_store(3, 1024, 1536)
+        score_out(2, 2)
+        score_store(2, 1024, 1536)
+        interleave_h(1, 1, nc.scalar.copy)
+        quant_h(1, 1)
+        diag_term(7, 0, nc.vector)
+        diag_term(7, 3, nc.gpsimd)
+        score_mm(1, 3)
+        tp(1, 0, 0)
+        tm(0, 0)
+        tp(1, 1, 1)
+        score_out(1, 3)
+        score_store(1, 1536, 2048)
+        evac_p(1, 1, 1)
+        diag_term(7, 1, nc.gpsimd)
+        score_out(2, 0)
+        score_store(2, 0, 512)
+        score_out(1, 2)
+        score_store(1, 1024, 1536)
+        score_mm(1, 1)
+        score_mm(7, 0)
+        score_out(1, 1)
+        score_store(1, 512, 1024)
+        diag_term(6, 2, nc.gpsimd)
+        score_mm(2, 1)
+        evac_m(0, 0)
+        evac_p(1, 0, 0)
+        score_mm(6, 2)
+        score_mm(6, 1)
+        tp(0, 1, 1)
+        score_out(7, 0)
+        score_store(7, 0, 512)
+        tp(0, 1, 0)
+        score_out(2, 1)
+        score_store(2, 512, 1024)
+        diag_term(6, 1, nc.vector)
+        score_out(6, 2)
+        score_store(6, 1024, 1536)
+        score_out(6, 1)
+        score_store(6, 512, 1024)
+        evac_p(0, 1, 1)
+        tm(0, 1)
+        tp(1, 1, 0)
+        evac_p(0, 1, 0)
+        diag_term(6, 0, nc.gpsimd)
+        tp(1, 0, 1)
+        score_mm(5, 1)
+        score_mm(5, 2)
+        score_mm(7, 1)
+        diag_term(6, 3, nc.vector)
+        quant_p(0, 1)
+        diag_term(5, 2, nc.vector)
+        diag_term(5, 1, nc.vector)
+        score_mm(6, 0)
+        score_mm(6, 3)
+        score_out(5, 2)
+        score_store(5, 1024, 1536)
+        score_out(5, 1)
+        score_store(5, 512, 1024)
+        score_out(6, 0)
+        score_store(6, 0, 512)
+        diag_term(4, 2, nc.gpsimd)
+        diag_term(7, 2, nc.gpsimd)
+        diag_term(4, 1, nc.gpsimd)
+        score_mm(4, 2)
+        evac_m(0, 1)
+        evac_p(1, 0, 1)
+        evac_p(1, 1, 0)
+        score_out(7, 1)
+        score_store(7, 512, 1024)
+        diag_term(5, 3, nc.gpsimd)
+        score_mm(7, 3)
+        score_mm(7, 2)
+        score_out(4, 2)
+        score_store(4, 1024, 1536)
+        score_out(6, 3)
+        score_store(6, 1536, 2048)
+        score_out(7, 2)
+        score_store(7, 1024, 1536)
+        score_out(7, 3)
+        score_store(7, 1536, 2048)
+        score_mm(4, 3)
+        diag_term(4, 3, nc.vector)
+        quant_m(0)
+        score_mm(4, 1)
+        quant_p(1, 1)
+        score_mm(5, 3)
+        score_out(4, 3)
+        score_store(4, 1536, 2048)
+        score_mm(4, 0)
+        score_mm(5, 0)
+        score_out(4, 1)
+        score_store(4, 512, 1024)
+        score_out(5, 3)
+        score_store(5, 1536, 2048)
+        diag_term(4, 0, nc.gpsimd)
+        profile_mm(0, 1)
+        profile_mm(2, 1)
+        profile_mm(1, 1)
+        score_out(4, 0)
+        score_store(4, 0, 512)
+        diag_term(5, 0, nc.gpsimd)
+        score_out(5, 0)
+        score_store(5, 0, 512)
+        quant_p(1, 0)
+        profile_out(2, 1)
+        profile_mm(3, 1)
+        profile_out(0, 1)
+        profile_mm(3, 0)
+        profile_mm(0, 0)
+        profile_mm(2, 0)
+        profile_out(1, 1)
+        profile_mm(1, 0)
+        profile_out(3, 1)
+        profile_out(3, 0)
+        profile_out(0, 0)
+        profile_out(2, 0)
+        profile_out(1, 0)

from contextlib import ExitStack

import concourse.mybir as mybir
from concourse.masks import make_identity

P = 128
B, I, R, C = 1024, 2048, 1024, 512
K_PASS = 512
N_TILE = 512
FLOPS = 2 * (B * I * R + B * R * I + C * B * R)

F32 = mybir.dt.float32
BF16 = mybir.dt.bfloat16
I32 = mybir.dt.int32
U32 = mybir.dt.uint32
U8 = mybir.dt.uint8
FP8 = mybir.dt.float8_e4m3fn
FP8X4 = mybir.dt.float8_e4m3fn_x4
FP4X4 = mybir.dt.float4_e2m1fn_x4
MULT = mybir.AluOpType.mult
SUB = mybir.AluOpType.subtract
COPY = mybir.ActivationFunctionType.Copy

ENC_SCALAR_PLANES = (3, 2)


def tile_lowrank_diagonal_recommender_s8_kernel(
    tc, x, enc_bytes, enc_scale, gain, dec_words, dec_scales, diag, mix, scores, profiles
):
    nc = tc.nc
    with ExitStack() as ctx:
        keep = ctx.enter_context(tc.tile_pool(name="keep", bufs=1))
        wide_pool = ctx.enter_context(tc.tile_pool(name="wide_pool", bufs=4))
        grp_pool = ctx.enter_context(tc.tile_pool(name="grp_pool", bufs=4))
        xg_pool = ctx.enter_context(tc.tile_pool(name="xg_pool", bufs=4))
        out_pool = ctx.enter_context(tc.tile_pool(name="out_pool", bufs=4))
        prof_pool = ctx.enter_context(tc.tile_pool(name="prof_pool", bufs=4))
        mm_psum = ctx.enter_context(tc.psum_pool(name="mm_psum", bufs=5))
        tr_psum = ctx.enter_context(tc.psum_pool(name="tr_psum", bufs=3))
        ctx.enter_context(tc.manual_schedule())

        ident = keep.tile([P, P], F32, name="ident")
        warm = keep.tile([P, 1], F32, name="warm")
        es = keep.tile([P, 4, 4], F32, name="es")
        gain_b = keep.tile([P, 2, 4], BF16, name="gain_b")
        gain_f = keep.tile([P, 2, 4], F32, name="gain_f")
        diag_b = keep.tile([P, I], BF16, name="diag_b")
        encb = [keep.tile([P, 4, R], U8, name=f"encb{g}", align_bytes=64) for g in range(4)]
        xt = [keep.tile([P, I], BF16, name=f"xt{b}", align_bytes=64) for b in range(8)]
        mixt = keep.tile([P, 4, B], BF16, name="mixt", align_bytes=64)
        encq = keep.tile([P, 4, R], U32, name="encq", align_bytes=64)
        encs = keep.tile([P, 4, R], U8, name="encs", align_bytes=64)
        xq = keep.tile([P, 4, B], U32, name="xq", align_bytes=64)
        xs = keep.tile([P, 4, B], U8, name="xs", align_bytes=64)
        hb = [[keep.tile([P, 4, 512], BF16, name=f"hb{c}{h}", align_bytes=64) for h in range(2)] for c in range(2)]
        hq = keep.tile([P, 2, B], U32, name="hq", align_bytes=64)
        hs = keep.tile([P, 2, B], U8, name="hs", align_bytes=64)
        pq = keep.tile([P, 2, R], U32, name="pq", align_bytes=64)
        ps = keep.tile([P, 2, R], U8, name="ps", align_bytes=64)
        mq = keep.tile([P, 2, C], U32, name="mq", align_bytes=64)
        ms = keep.tile([P, 2, C], U8, name="ms", align_bytes=64)
        ww = keep.tile([P, 2, 2 * I], U8, name="ww", align_bytes=64)
        ws = keep.tile([P, 2, I], U8, name="ws", align_bytes=64)

        nc.scalar.dma_start(out=es[:], in_=enc_scale.rearrange("(g p t) o -> p g (t o)", p=P, t=4))
        nc.scalar.dma_start(out=gain_b[:], in_=gain.rearrange("(h p t) -> p h t", p=P, t=4))
        enc_v = enc_bytes.rearrange("(g p t) n -> g p t n", p=P, t=4)

        def load_enc(g):
            nc.sync.dma_start(out=encb[g][:], in_=enc_v[g])

        def load_x(b):
            nc.sync.dma_start(out=xt[b][:], in_=x[b * P : (b + 1) * P, :])

        load_enc(0)
        load_x(0)
        load_x(1)
        load_enc(1)
        load_x(2)
        load_x(3)
        load_enc(2)
        load_enc(3)
        for b in range(4, 8):
            load_x(b)
        nc.sync.dma_start(out=ww[:], in_=dec_words.rearrange("g p n -> p g n"))
        nc.gpsimd.memset(ws[:].rearrange("p g n -> p (g n)").bitcast(I32), 0)
        make_identity(nc, ident[:])
        ws_words = ws[:].rearrange("p g n -> p (g n)").bitcast(I32)
        for r in range(4):
            nc.sync.dma_start(
                out=ws_words[r:P:32, :].rearrange("q (g n) -> q g n", g=2),
                in_=dec_scales.rearrange("g (q r) n -> r q g n", r=4)[r].bitcast(I32),
            )
        nc.sync.dma_start(out=diag_b[:], in_=diag.partition_broadcast(P))
        nc.sync.dma_start(out=mixt[:], in_=mix.rearrange("(c p) b -> p c b", p=P))

        nc.vector.memset(warm[:], 0.0)
        nc.scalar.activation(out=warm[:], in_=warm[:], func=COPY, scale=1.0)
        nc.vector.tensor_copy(out=gain_f[:], in_=gain_b[:])

        wide = {}
        grouped = {}

        def widen_plane(h, g, j, engine_is_scalar):
            if (h, g) not in wide:
                wide[h, g] = wide_pool.tile([P, 4, 512], BF16, name="wide", align_bytes=64)
            src = encb[g][:, j, h * 512 : (h + 1) * 512].bitcast(FP8)
            dst = wide[h, g][:, j, :]
            if engine_is_scalar:
                nc.scalar.activation(out=dst, in_=src, func=COPY, scale=es[:, g, j : j + 1])
            else:
                nc.vector.tensor_scalar(out=dst, in0=src, scalar1=es[:, g, j : j + 1], scalar2=None, op0=MULT)

        def widen(h, g):
            for j in range(4):
                widen_plane(h, g, j, j < ENC_SCALAR_PLANES[h])

        def interleave_enc(h, g, copy):
            grouped["e", h, g] = grp_pool.tile([P, 512, 4], BF16, name="grp", align_bytes=64)
            copy(
                out=grouped["e", h, g][:].rearrange("p (t m) j -> p m j t", t=4),
                in_=wide[h, g][:].rearrange("p j (m t) -> p m j t", t=4),
            )

        def quant_enc(h, g):
            nc.vector.quantize_mx(
                out=encq[:, g, h * 512 : (h + 1) * 512].bitcast(FP8X4),
                scales=encs[:, g, h * 512 : (h + 1) * 512],
                in_=grouped["e", h, g][:].rearrange("p n j -> p (n j)"),
            )

        banks = {}
        xg = {}

        def tx(q, g):
            banks["x", q, g] = tr_psum.tile([P, 2, 2, P], F32, name="tr")
            for k in range(2):
                words = xt[2 * q + k][:].bitcast(F32)
                for u in range(2):
                    nc.tensor.transpose(
                        banks["x", q, g][:, k, u, :], words[:, 256 * g + u : 256 * (g + 1) : 2], ident[:]
                    )

        def evac_x(q, g, copy):
            xg[q, g] = xg_pool.tile([P, 256, 4], BF16, name="xg", align_bytes=64)
            copy(
                out=xg[q, g][:].rearrange("p (k r) t -> p k (r t)", k=2).bitcast(F32).rearrange("p k (r u) -> p k r u", u=2),
                in_=banks["x", q, g][:].rearrange("p k u r -> p k r u"),
            )

        def quant_x(q, g):
            nc.vector.quantize_mx(
                out=xq[:, g, q * 256 : (q + 1) * 256].bitcast(FP8X4),
                scales=xs[:, g, q * 256 : (q + 1) * 256],
                in_=xg[q, g][:].rearrange("p n j -> p (n j)"),
            )

        h_ps = {}

        def h_pass(c, h, t, g):
            if g == 0:
                h_ps[c, h, t] = mm_psum.tile([P, N_TILE], F32, name="mm")
            lo = h * 512 + t * P
            nc.tensor.matmul_mx(
                out=h_ps[c, h, t][:],
                lhsT=encq[:, g, lo : lo + P].bitcast(FP8X4),
                lhsT_scale=encs[:, g, lo : lo + P],
                rhs=xq[:, g, c * 512 : (c + 1) * 512].bitcast(FP8X4),
                rhs_scale=xs[:, g, c * 512 : (c + 1) * 512],
                start=(g == 0),
                stop=(g == 3),
            )

        def evac_h(c, h, t, engine_is_scalar):
            if engine_is_scalar:
                nc.scalar.activation(
                    out=hb[c][h][:, t, :], in_=h_ps[c, h, t][:], func=COPY, scale=gain_f[:, h, t : t + 1]
                )
            else:
                nc.vector.tensor_scalar(
                    out=hb[c][h][:, t, :], in0=h_ps[c, h, t][:], scalar1=gain_f[:, h, t : t + 1], scalar2=None, op0=MULT
                )

        def interleave_h(c, h, copy):
            grouped["h", c, h] = grp_pool.tile([P, 512, 4], BF16, name="grp", align_bytes=64)
            copy(
                out=grouped["h", c, h][:].rearrange("p (k i) t -> p k t i", i=4),
                in_=hb[c][h][:].rearrange("p t (k i) -> p k t i", i=4),
            )

        def quant_h(c, h):
            nc.vector.quantize_mx(
                out=hq[:, h, c * 512 : (c + 1) * 512].bitcast(FP8X4),
                scales=hs[:, h, c * 512 : (c + 1) * 512],
                in_=grouped["h", c, h][:].rearrange("p n j -> p (n j)"),
            )

        def tp(c, h, k):
            banks["p", c, h, k] = tr_psum.tile([P, 2, 2, P], F32, name="tr")
            for i in range(2):
                words = hb[c][h][:, 2 * k + i, :].bitcast(F32)
                for u in range(2):
                    nc.tensor.transpose(banks["p", c, h, k][:, i, u, :], words[:, u:256:2], ident[:])

        def evac_p(c, h, k):
            if ("p", c, h) not in grouped:
                grouped["p", c, h] = grp_pool.tile([P, 512, 4], BF16, name="grp", align_bytes=64)
            half = grouped["p", c, h][:, k * 256 : (k + 1) * 256, :]
            nc.scalar.copy(
                out=half.rearrange("p n t -> p (n t)").bitcast(F32).rearrange("p (i r u) -> p i r u", i=2, u=2),
                in_=banks["p", c, h, k][:].rearrange("p i u r -> p i r u"),
            )

        def quant_p(c, h):
            nc.vector.quantize_mx(
                out=pq[:, c, h * 512 : (h + 1) * 512].bitcast(FP8X4),
                scales=ps[:, c, h * 512 : (h + 1) * 512],
                in_=grouped["p", c, h][:].rearrange("p n j -> p (n j)"),
            )

        def tm(c, k):
            banks["m", c, k] = tr_psum.tile([P, 2, 2, P], F32, name="tr")
            for i in range(2):
                words = mixt[:, 2 * k + i, :].bitcast(F32)
                for u in range(2):
                    nc.tensor.transpose(
                        banks["m", c, k][:, i, u, :], words[:, 256 * c + u : 256 * (c + 1) : 2], ident[:]
                    )

        def evac_m(c, k):
            if ("m", c) not in grouped:
                grouped["m", c] = grp_pool.tile([P, 512, 4], BF16, name="grp", align_bytes=64)
            half = grouped["m", c][:, k * 256 : (k + 1) * 256, :]
            nc.scalar.copy(
                out=half.rearrange("p n t -> p (n t)").bitcast(F32).rearrange("p (i r u) -> p i r u", i=2, u=2),
                in_=banks["m", c, k][:].rearrange("p i u r -> p i r u"),
            )

        def quant_m(c):
            nc.vector.quantize_mx(
                out=mq[:, c, :].bitcast(FP8X4),
                scales=ms[:, c, :],
                in_=grouped["m", c][:].rearrange("p n j -> p (n j)"),
            )

        ot = {}

        def diag_term(b, n, engine):
            if b not in ot:
                ot[b] = out_pool.tile([P, I], F32, name="ot", align_bytes=64)
            cols = slice(n * N_TILE, (n + 1) * N_TILE)
            engine.tensor_tensor(out=ot[b][:, cols], in0=xt[b][:, cols], in1=diag_b[:, cols], op=MULT)

        s_ps = {}

        def score_mm(b, n):
            s_ps[b, n] = mm_psum.tile([P, N_TILE], F32, name="mm")
            cols = slice(n * N_TILE, (n + 1) * N_TILE)
            for h in range(2):
                nc.tensor.matmul_mx(
                    out=s_ps[b, n][:],
                    lhsT=hq[:, h, b * P : (b + 1) * P].bitcast(FP8X4),
                    lhsT_scale=hs[:, h, b * P : (b + 1) * P],
                    rhs=ww[:, h, n * 2 * N_TILE : (n + 1) * 2 * N_TILE].bitcast(FP4X4),
                    rhs_scale=ws[:, h, cols],
                    start=(h == 0),
                    stop=(h == 1),
                )

        def score_out(b, n):
            cols = slice(n * N_TILE, (n + 1) * N_TILE)
            nc.vector.tensor_tensor(out=ot[b][:, cols], in0=s_ps[b, n][:], in1=ot[b][:, cols], op=SUB)

        def score_store(b, lo, hi):
            nc.sync.dma_start(out=scores[b * P : (b + 1) * P, lo:hi], in_=ot[b][:, lo:hi])

        p_ps = {}
        pt = {}

        def profile_mm(m, h):
            p_ps[m, h] = mm_psum.tile([P, N_TILE], F32, name="mm")
            for c in range(2):
                nc.tensor.matmul_mx(
                    out=p_ps[m, h][:],
                    lhsT=mq[:, c, m * P : (m + 1) * P].bitcast(FP8X4),
                    lhsT_scale=ms[:, c, m * P : (m + 1) * P],
                    rhs=pq[:, c, h * 512 : (h + 1) * 512].bitcast(FP8X4),
                    rhs_scale=ps[:, c, h * 512 : (h + 1) * 512],
                    start=(c == 0),
                    stop=(c == 1),
                )

        def profile_out(m, h):
            piece = prof_pool.tile([P, N_TILE], F32, name="piece", align_bytes=64)
            nc.scalar.copy(
                out=piece[:].rearrange("p (r t) -> p r t", t=4), in_=p_ps[m, h][:].rearrange("p (t r) -> p r t", t=4)
            )
            nc.sync.dma_start(out=profiles[m * P : (m + 1) * P, h * 512 : (h + 1) * 512], in_=piece[:])

        widen_plane(0, 0, 0, False)
        widen_plane(1, 0, 2, False)
        widen_plane(1, 0, 1, True)
        widen_plane(0, 0, 2, True)
        tx(0, 3)
        tx(0, 2)
        widen_plane(0, 0, 3, False)
        widen_plane(0, 0, 1, False)
        tx(0, 0)
        widen_plane(1, 0, 3, True)
        widen_plane(1, 0, 0, False)
        interleave_enc(0, 0, nc.vector.tensor_copy)
        evac_x(0, 3, nc.vector.tensor_copy)
        widen_plane(0, 1, 1, False)
        widen_plane(0, 1, 2, False)
        widen_plane(0, 1, 0, False)
        quant_x(0, 3)
        interleave_enc(1, 0, nc.scalar.copy)
        evac_x(0, 2, nc.scalar.copy)
        quant_enc(1, 0)
        quant_x(0, 2)
        tx(0, 1)
        tx(1, 3)
        evac_x(0, 1, nc.scalar.copy)
        evac_x(0, 0, nc.scalar.copy)
        quant_enc(0, 0)
        tx(1, 0)
        evac_x(1, 3, nc.scalar.copy)
        widen_plane(0, 2, 2, False)
        widen_plane(1, 2, 2, False)
        widen_plane(0, 1, 3, True)
        quant_x(0, 1)
        interleave_enc(0, 1, nc.vector.tensor_copy)
        widen_plane(1, 1, 1, False)
        widen_plane(0, 2, 0, False)
        quant_x(0, 0)
        widen_plane(0, 3, 0, False)
        widen_plane(1, 1, 0, True)
        evac_x(1, 0, nc.scalar.copy)
        tx(1, 1)
        evac_x(1, 1, nc.scalar.copy)
        quant_x(1, 1)
        quant_x(1, 3)
        quant_x(1, 0)
        widen_plane(0, 2, 3, False)
        quant_enc(0, 1)
        widen_plane(0, 3, 2, False)
        widen_plane(0, 3, 3, True)
        tx(2, 0)
        widen_plane(1, 2, 0, True)
        tx(2, 3)
        tx(1, 2)
        evac_x(2, 0, nc.scalar.copy)
        widen_plane(0, 2, 1, True)
        evac_x(2, 3, nc.scalar.copy)
        tx(3, 0)
        evac_x(1, 2, nc.scalar.copy)
        tx(3, 1)
        widen_plane(0, 3, 1, False)
        evac_x(3, 0, nc.scalar.copy)
        quant_x(2, 0)
        quant_x(2, 3)
        widen_plane(1, 1, 3, False)
        interleave_enc(0, 2, nc.vector.tensor_copy)
        tx(2, 2)
        evac_x(3, 1, nc.scalar.copy)
        quant_x(3, 0)
        tx(3, 2)
        tx(2, 1)
        quant_x(1, 2)
        interleave_enc(0, 3, nc.scalar.copy)
        evac_x(3, 2, nc.scalar.copy)
        widen_plane(1, 3, 0, True)
        quant_enc(0, 2)
        evac_x(2, 1, nc.scalar.copy)
        quant_enc(0, 3)
        h_pass(0, 0, 3, 0)
        h_pass(0, 0, 0, 0)
        h_pass(0, 0, 1, 0)
        widen_plane(1, 2, 1, False)
        h_pass(0, 0, 1, 1)
        h_pass(0, 0, 2, 0)
        widen_plane(1, 1, 2, False)
        h_pass(0, 0, 2, 1)
        h_pass(0, 0, 3, 1)
        h_pass(0, 0, 0, 1)
        h_pass(0, 0, 1, 2)
        h_pass(0, 0, 0, 2)
        h_pass(0, 0, 3, 2)
        h_pass(0, 0, 1, 3)
        diag_term(0, 0, nc.vector)
        h_pass(0, 0, 0, 3)
        h_pass(0, 0, 2, 2)
        h_pass(0, 0, 3, 3)
        quant_x(2, 1)
        interleave_enc(1, 1, nc.vector.tensor_copy)
        evac_x(2, 2, nc.scalar.copy)
        h_pass(1, 0, 0, 0)
        quant_x(3, 1)
        evac_h(0, 0, 0, True)
        tx(3, 3)
        tm(1, 1)
        evac_h(0, 0, 3, True)
        evac_h(0, 0, 1, True)
        evac_x(3, 3, nc.scalar.copy)
        tm(1, 0)
        h_pass(0, 0, 2, 3)
        widen_plane(1, 2, 3, False)
        widen_plane(1, 3, 1, True)
        widen_plane(1, 3, 2, True)
        quant_x(2, 2)
        widen_plane(1, 3, 3, False)
        quant_x(3, 2)
        evac_m(1, 1)
        evac_h(0, 0, 2, True)
        diag_term(3, 0, nc.vector)
        quant_x(3, 3)
        diag_term(1, 0, nc.vector)
        quant_enc(1, 1)
        diag_term(1, 1, nc.vector)
        evac_m(1, 0)
        h_pass(1, 0, 3, 0)
        h_pass(1, 0, 0, 1)
        h_pass(1, 0, 2, 0)
        h_pass(0, 1, 3, 0)
        h_pass(1, 0, 2, 1)
        h_pass(1, 0, 2, 2)
        h_pass(1, 0, 0, 2)
        h_pass(1, 0, 3, 1)
        h_pass(1, 0, 3, 2)
        h_pass(1, 0, 2, 3)
        h_pass(1, 0, 1, 0)
        h_pass(1, 0, 0, 3)
        interleave_enc(1, 2, nc.vector.tensor_copy)
        evac_h(1, 0, 0, False)
        h_pass(1, 0, 3, 3)
        evac_h(1, 0, 2, True)
        tp(0, 0, 1)
        tp(0, 0, 0)
        h_pass(1, 0, 1, 1)
        evac_h(1, 0, 3, False)
        diag_term(0, 2, nc.gpsimd)
        quant_enc(1, 2)
        h_pass(1, 0, 1, 2)
        h_pass(1, 0, 1, 3)
        h_pass(0, 1, 3, 1)
        h_pass(0, 1, 0, 0)
        h_pass(0, 1, 0, 1)
        h_pass(0, 1, 2, 0)
        h_pass(0, 1, 3, 2)
        h_pass(0, 1, 2, 1)
        interleave_enc(1, 3, nc.scalar.copy)
        interleave_h(0, 0, nc.scalar.copy)
        quant_enc(1, 3)
        diag_term(2, 3, nc.vector)
        quant_m(1)
        h_pass(0, 1, 0, 2)
        h_pass(0, 1, 3, 3)
        h_pass(0, 1, 0, 3)
        h_pass(0, 1, 1, 0)
        h_pass(0, 1, 2, 2)
        h_pass(0, 1, 1, 1)
        h_pass(0, 1, 1, 2)
        h_pass(0, 1, 2, 3)
        diag_term(3, 2, nc.vector)
        evac_h(1, 0, 1, False)
        evac_h(0, 1, 3, True)
        diag_term(3, 1, nc.gpsimd)
        h_pass(1, 1, 1, 0)
        h_pass(0, 1, 1, 3)
        h_pass(1, 1, 0, 0)
        h_pass(1, 1, 1, 1)
        evac_h(0, 1, 2, False)
        evac_h(0, 1, 0, True)
        h_pass(1, 1, 0, 1)
        diag_term(0, 3, nc.vector)
        h_pass(1, 1, 3, 0)
        h_pass(1, 1, 2, 0)
        h_pass(1, 1, 2, 1)
        h_pass(1, 1, 2, 2)
        h_pass(1, 1, 2, 3)
        h_pass(1, 1, 0, 2)
        h_pass(1, 1, 1, 2)
        h_pass(1, 1, 1, 3)
        h_pass(1, 1, 3, 1)
        h_pass(1, 1, 3, 2)
        h_pass(1, 1, 3, 3)
        evac_p(0, 0, 1)
        evac_h(0, 1, 1, True)
        quant_h(0, 0)
        evac_p(0, 0, 0)
        interleave_h(1, 0, nc.scalar.copy)
        h_pass(1, 1, 0, 3)
        interleave_h(0, 1, nc.vector.tensor_copy)
        evac_h(1, 1, 1, True)
        diag_term(3, 3, nc.vector)
        quant_h(0, 1)
        evac_h(1, 1, 0, True)
        score_mm(0, 3)
        score_mm(0, 0)
        evac_h(1, 1, 3, True)
        evac_h(1, 1, 2, True)
        quant_p(0, 0)
        quant_h(1, 0)
        score_out(0, 3)
        score_store(0, 1536, 2048)
        score_out(0, 0)
        score_store(0, 0, 512)
        diag_term(0, 1, nc.gpsimd)
        diag_term(2, 1, nc.gpsimd)
        score_mm(3, 1)
        score_mm(0, 1)
        score_mm(0, 2)
        score_mm(3, 3)
        diag_term(1, 3, nc.gpsimd)
        score_out(3, 1)
        score_store(3, 512, 1024)
        score_out(0, 1)
        score_store(0, 512, 1024)
        diag_term(1, 2, nc.gpsimd)
        score_out(0, 2)
        score_store(0, 1024, 1536)
        score_out(3, 3)
        score_store(3, 1536, 2048)
        score_mm(1, 0)
        score_out(1, 0)
        score_store(1, 0, 512)
        diag_term(2, 2, nc.gpsimd)
        score_mm(3, 0)
        score_mm(2, 3)
        score_mm(3, 2)
        score_out(2, 3)
        score_store(2, 1536, 2048)
        score_out(3, 0)
        score_store(3, 0, 512)
        diag_term(2, 0, nc.gpsimd)
        score_mm(2, 0)
        score_mm(2, 2)
        score_mm(1, 2)
        score_out(3, 2)
        score_store(3, 1024, 1536)
        score_out(2, 2)
        score_store(2, 1024, 1536)
        interleave_h(1, 1, nc.scalar.copy)
        quant_h(1, 1)
        diag_term(7, 0, nc.vector)
        diag_term(7, 3, nc.gpsimd)
        score_mm(1, 3)
        tp(1, 0, 0)
        tm(0, 0)
        tp(1, 1, 1)
        score_out(1, 3)
        score_store(1, 1536, 2048)
        evac_p(1, 1, 1)
        diag_term(7, 1, nc.gpsimd)
        score_out(2, 0)
        score_store(2, 0, 512)
        score_out(1, 2)
        score_store(1, 1024, 1536)
        score_mm(1, 1)
        score_mm(7, 0)
        score_out(1, 1)
        score_store(1, 512, 1024)
        diag_term(6, 2, nc.gpsimd)
        score_mm(2, 1)
        evac_m(0, 0)
        evac_p(1, 0, 0)
        score_mm(6, 2)
        score_mm(6, 1)
        tp(0, 1, 1)
        score_out(7, 0)
        score_store(7, 0, 512)
        tp(0, 1, 0)
        score_out(2, 1)
        score_store(2, 512, 1024)
        diag_term(6, 1, nc.vector)
        score_out(6, 2)
        score_store(6, 1024, 1536)
        score_out(6, 1)
        score_store(6, 512, 1024)
        evac_p(0, 1, 1)
        tm(0, 1)
        tp(1, 1, 0)
        evac_p(0, 1, 0)
        diag_term(6, 0, nc.gpsimd)
        tp(1, 0, 1)
        score_mm(5, 1)
        score_mm(5, 2)
        score_mm(7, 1)
        diag_term(6, 3, nc.vector)
        quant_p(0, 1)
        diag_term(5, 2, nc.vector)
        diag_term(5, 1, nc.vector)
        score_mm(6, 0)
        score_mm(6, 3)
        score_out(5, 2)
        score_store(5, 1024, 1536)
        score_out(5, 1)
        score_store(5, 512, 1024)
        score_out(6, 0)
        score_store(6, 0, 512)
        diag_term(4, 2, nc.gpsimd)
        diag_term(7, 2, nc.gpsimd)
        diag_term(4, 1, nc.gpsimd)
        score_mm(4, 2)
        evac_m(0, 1)
        evac_p(1, 0, 1)
        evac_p(1, 1, 0)
        score_out(7, 1)
        score_store(7, 512, 1024)
        diag_term(5, 3, nc.gpsimd)
        score_mm(7, 3)
        score_mm(7, 2)
        score_out(4, 2)
        score_store(4, 1024, 1536)
        score_out(6, 3)
        score_store(6, 1536, 2048)
        score_out(7, 2)
        score_store(7, 1024, 1536)
        score_out(7, 3)
        score_store(7, 1536, 2048)
        score_mm(4, 3)
        diag_term(4, 3, nc.vector)
        quant_m(0)
        score_mm(4, 1)
        quant_p(1, 1)
        score_mm(5, 3)
        score_out(4, 3)
        score_store(4, 1536, 2048)
        score_mm(4, 0)
        score_mm(5, 0)
        score_out(4, 1)
        score_store(4, 512, 1024)
        score_out(5, 3)
        score_store(5, 1536, 2048)
        diag_term(4, 0, nc.gpsimd)
        profile_mm(0, 1)
        profile_mm(2, 1)
        profile_mm(1, 1)
        score_out(4, 0)
        score_store(4, 0, 512)
        diag_term(5, 0, nc.gpsimd)
        score_out(5, 0)
        score_store(5, 0, 512)
        quant_p(1, 0)
        profile_out(2, 1)
        profile_mm(3, 1)
        profile_out(0, 1)
        profile_mm(3, 0)
        profile_mm(0, 0)
        profile_mm(2, 0)
        profile_out(1, 1)
        profile_mm(1, 0)
        profile_out(3, 1)
        profile_out(3, 0)
        profile_out(0, 0)
        profile_out(2, 0)
        profile_out(1, 0)
